import numpy as np
import ml_dtypes


def mxq(x, axis, fmt="e4m3"):
    dtype, down = {"e4m3": (ml_dtypes.float8_e4m3fn, 7), "e5m2": (ml_dtypes.float8_e5m2, 14)}[fmt]
    v = np.moveaxis(np.asarray(x, np.float32).astype(ml_dtypes.bfloat16).astype(np.float64), axis, -1)
    blocks = v.reshape(v.shape[:-1] + (-1, 32))
    amax = np.abs(blocks).max(-1, keepdims=True)
    byte = np.maximum(np.where(amax > 0, np.frexp(amax)[1] - 1 + 127, 0) - down, 1)
    scale = np.exp2(byte - 127.0)
    codes = (blocks / scale).astype(np.float32).astype(dtype).astype(np.float64)
    return np.moveaxis((codes * scale).reshape(v.shape), -1, axis)


WIDE = False


def mx_kscale(k):
    if not WIDE:
        return np.ones(k)
    levels = np.array([10, -10, 5, -5, 0])
    if k % 512:
        return np.exp2(np.random.permutation(np.resize(levels, k // 32))).repeat(32)
    a = np.empty((k // 512, 16))
    for p in range(k // 512):
        a[p, :8] = np.random.permutation(np.resize(levels, 8))
        for g in range(8):
            far = levels[np.abs(levels - a[p, g]) >= 10]
            a[p, g + 8] = far[np.random.randint(len(far))]
    return np.exp2(a.ravel()).repeat(32)


def f64(x):
    return np.asarray(x).astype(np.float64)


def striped(idx):
    return np.tile(np.asarray(idx).reshape(-1, 16).T, (8, 1)).astype(np.uint16)


def unstriped(offs):
    return offs[:16].T.reshape(-1).astype(np.int64)


def striped8(idx):
    return np.asarray(idx).reshape(8, -1, 16).transpose(0, 2, 1).reshape(128, -1).astype(np.uint16)


def unstriped8(offs):
    return offs.reshape(8, 16, -1).transpose(0, 2, 1).reshape(8, -1).astype(np.int64)


def pick8(x, idx, run):
    r = np.arange(len(x))
    return x[r[:, None], idx[r % (8 * run) // run]]


E2M1 = np.array([0.0, 0.5, 1.0, 1.5, 2.0, 3.0, 4.0, 6.0, -0.0, -0.5, -1.0, -1.5, -2.0, -3.0, -4.0, -6.0])


def pack_weight(w, fmt):
    k, n = w.shape
    w = f64(np.asarray(w, np.float32).astype(ml_dtypes.bfloat16)).reshape(k // 32, 32, n)
    amax = np.abs(w).max(1)
    if fmt == "e4m3":
        byte = np.frexp(amax)[1] - 1 + 127 - 7
    else:
        mant, ex = np.frexp(amax / 6.0)
        byte = np.where(mant > 0.5, ex, ex - 1) + 127
    byte = np.clip(np.where(amax > 0, byte, 1), 1, 254)
    scaled = (w * np.exp2(127.0 - byte)[:, None, :]).reshape(k, n).astype(np.float32)
    by_word = np.ascontiguousarray(scaled.reshape(k // 512, 128, 4, n).transpose(0, 1, 3, 2))
    if fmt == "e4m3":
        words = by_word.astype(ml_dtypes.float8_e4m3fn).view(np.uint8)
    else:
        c = by_word.astype(ml_dtypes.float4_e2m1fn).view(np.uint8) & 0xF
        words = (c[..., 0::2] | (c[..., 1::2] << 4)).reshape(k // 512, 128, 2 * n)
    return np.ascontiguousarray(words), np.ascontiguousarray(byte.astype(np.uint8).reshape(k // 512, 16, n))


def unpack_weight(words, scales, fmt):
    g, _, n = scales.shape
    words = np.ascontiguousarray(words).reshape(g, 128, n, -1)
    if fmt == "e4m3":
        vals = words.view(ml_dtypes.float8_e4m3fn).astype(np.float64)
    else:
        nib = np.empty((g, 128, n, 4), np.uint8)
        nib[..., 0::2] = words & 0xF
        nib[..., 1::2] = words >> 4
        vals = E2M1[nib]
    vals = vals * np.repeat(np.exp2(scales.astype(np.float64) - 127.0), 8, axis=1)[..., None]
    return vals.transpose(0, 1, 3, 2).reshape(g * 512, n)


K, J, R, T, C, O, U, D, N, S = 512, 256, 512, 1024, 512, 128, 128, 256, 256, 1024


def setup_inputs():
    n = np.random.standard_normal
    idx = np.random.permutation(T)[:J]
    idx2 = np.stack([np.random.permutation(C)[:J] for _ in range(8)])
    idx3 = np.stack([np.random.permutation(C)[:J] for _ in range(8)])
    idx4 = np.stack([np.random.permutation(C)[:O] for _ in range(8)])
    idx5 = np.stack([np.random.permutation(C)[:U] for _ in range(8)])
    idx6 = np.random.permutation(S)[:N]
    fk = mx_kscale(K)
    fr = mx_kscale(R)
    xtp = pack_weight(n((K, T)) * fk[:, None], "e4m3")
    wp = pack_weight(n((K, R)) * 1 / np.sqrt(K) / fk[:, None] * fr, "e4m3")
    w2p = pack_weight(n((K, R)) * 1 / np.sqrt(K) / fk[:, None] * fr, "e2m1")
    vsp = pack_weight(n((R, S)) * 1 / np.sqrt(R) / fr[:, None], "e2m1")
    return {
        "xt_words": xtp[0],
        "xt_scales": xtp[1],
        "w_words": wp[0],
        "w_scales": wp[1],
        "w2_words": w2p[0],
        "w2_scales": w2p[1],
        "sa": (np.random.uniform(0.5, 1.6, (R, 1))).astype(np.float32),
        "sb": (np.random.uniform(0.5, 1.6, (R, 1))).astype(np.float32),
        "vs_words": vsp[0],
        "vs_scales": vsp[1],
        "offs": striped(idx),
        "offs2": striped8(idx2),
        "offs3": striped8(idx3),
        "offs4": striped8(idx4),
        "offs5": striped8(idx5),
        "offs6": striped(idx6),
    }


def reference(xt_words, xt_scales, w_words, w_scales, w2_words, w2_scales, sa, sb, vs_words, vs_scales, offs, offs2, offs3, offs4, offs5, offs6):
    idx = unstriped(offs)
    idx2 = unstriped8(offs2)
    idx3 = unstriped8(offs3)
    idx4 = unstriped8(offs4)
    idx5 = unstriped8(offs5)
    idx6 = unstriped(offs6)
    xtu = unpack_weight(xt_words, xt_scales, "e4m3")
    wu = unpack_weight(w_words, w_scales, "e4m3")
    w2u = unpack_weight(w2_words, w2_scales, "e2m1")
    vsu = unpack_weight(vs_words, vs_scales, "e2m1")
    xtidxg = xtu[:, idx]
    a = wu.T @ xtidxg
    b = w2u.T @ xtidxg
    pw = np.zeros((R, C))
    pw[np.arange(R)[:, None], idx2[np.arange(R) % 512 // 64]] = a
    pv = np.zeros((R, C))
    pv[np.arange(R)[:, None], idx3[np.arange(R) % 512 // 64]] = b
    ph = np.maximum(pw, pv)
    pl = np.minimum(pw, pv)
    h1 = pick8(ph, idx4, 64) * f64(sa)
    h2 = pick8(pl, idx5, 64) * f64(sb)
    hid = np.concatenate([h1, h2], axis=1)
    vsidx6g = vsu[:, idx6]
    hidq = mxq(hid, 0, "e4m3")
    y = vsidx6g.T @ hidq
    return y

@@ -1,0 +1,215 @@
+from contextlib import ExitStack
+
+import concourse.mybir as mybir
+
+K, J, R, T, C, O, U, D, N, S = 512, 256, 512, 1024, 512, 128, 128, 256, 256, 1024
+FLOPS = 2 * K * R * J * 2 + 2 * R * N * D
+
+F32 = mybir.dt.float32
+BF16 = mybir.dt.bfloat16
+I32 = mybir.dt.int32
+U32 = mybir.dt.uint32
+U16 = mybir.dt.uint16
+U8 = mybir.dt.uint8
+FP8X4 = mybir.dt.float8_e4m3fn_x4
+FP4X4 = mybir.dt.float4_e2m1fn_x4
+COPY = mybir.ActivationFunctionType.Copy
+MAX = mybir.AluOpType.max
+MIN = mybir.AluOpType.min
+
+P = 128
+PACK = 4
+QUAD = 32
+HALF = J // 2
+PER_COL = 16
+
+
+def tile_picked_tokens_plain_twin_winnersides_store_plain_kernel(
+    tc, xt_words, xt_scales, w_words, w_scales, w2_words, w2_scales, sa, sb, vs_words, vs_scales,
+    offs, offs2, offs3, offs4, offs5, offs6, out,
+):
+    nc = tc.nc
+    with ExitStack() as ctx:
+        lists = ctx.enter_context(tc.tile_pool(name="lists", bufs=1))
+        keep = ctx.enter_context(tc.tile_pool(name="keep", bufs=1))
+        psum = ctx.enter_context(tc.psum_pool(name="psum", bufs=4))
+        psum_out = ctx.enter_context(tc.psum_pool(name="psum_out", bufs=1))
+
+        def load_list(src, name):
+            tile = lists.tile(list(src.shape), U16, name=name)
+            nc.sync.dma_start(tile[:], src)
+            return tile
+
+        def zeroed_plane(width, name, tag=""):
+            plane = keep.tile([P, width], U8, name=name, align_bytes=64, tag=tag)
+            nc.vector.memset(plane[:].bitcast(I32), 0)
+            return plane
+
+        def load_plane_rows(queue, plane, scales, quads):
+            rows = scales[0].bitcast(I32)
+            for q in quads:
+                queue.dma_start(plane[QUAD * q : QUAD * q + PACK, :].bitcast(I32), rows[PACK * q : PACK * (q + 1), :])
+
+        def load_staged_rows(queue, scales, name):
+            staged = keep.tile([PACK, P // QUAD, R // 4], I32, name=name)
+            queue.dma_start(staged[:], scales[0].bitcast(I32).rearrange("(q i) c -> i q c", i=PACK))
+            return staged
+
+        def spread_rows(plane, staged):
+            for q in range(P // QUAD):
+                nc.vector.tensor_copy(plane[QUAD * q : QUAD * q + PACK, :].bitcast(I32), staged[:, q, :])
+
+        xs_all = zeroed_plane(T, "xs_all", "xs_all")
+        w2s_all = zeroed_plane(R, "w2s_all", "w2s_all")
+
+        ws_all = zeroed_plane(R, "ws_all", "ws_all")
+
+        idx = load_list(offs, "idx")
+        w2s_staged = load_staged_rows(nc.scalar, w2_scales, "w2s_staged")
+        load_plane_rows(nc.scalar, xs_all, xt_scales, (1, 2, 3))
+        w2w_all = keep.tile([P, 2 * R], U8, name="w2w_all", align_bytes=64, tag="w2w_all")
+        nc.sync.dma_start(w2w_all[:].bitcast(I32), w2_words[0].bitcast(I32))
+        load_plane_rows(nc.sync, xs_all, xt_scales, (0,))
+        xw_all = keep.tile([P, T], I32, name="xw_all", align_bytes=64, tag="xw_all")
+        nc.sync.dma_start(xw_all[:], xt_words[0].rearrange("p c t -> p (c t)").bitcast(I32))
+        idx3 = load_list(offs3, "idx3")
+        ws_staged = load_staged_rows(nc.sync, w_scales, "ws_staged")
+        ww_all = keep.tile([P, R], I32, name="ww_all", align_bytes=64, tag="ww_all")
+        nc.sync.dma_start(ww_all[:], w_words[0].rearrange("p c t -> p (c t)").bitcast(I32))
+        idx2 = load_list(offs2, "idx2")
+
+        boards = {}
+        for name in ("pv0", "pv1", "pw0", "pw1"):
+            boards[name] = keep.tile([P, C], F32, name=name)
+            nc.vector.memset(boards[name][:], 0.0)
+
+        vss_all = zeroed_plane(S, "vss_all")
+        idx6 = load_list(offs6, "idx6")
+        vsw_all = keep.tile([P, S], U16, name="vsw_all")
+        nc.sync.dma_start(vsw_all[:].bitcast(I32), vs_words[0].bitcast(I32))
+        load_plane_rows(nc.sync, vss_all, vs_scales, range(P // QUAD))
+        idx4 = load_list(offs4, "idx4")
+        idx5 = load_list(offs5, "idx5")
+        sa_sb = keep.tile([P, PACK], F32, name="sa_sb")
+        nc.sync.dma_start(sa_sb[:], sa.rearrange("(p t) o -> p (t o)", t=PACK))
+        sb_sb = keep.tile([P, PACK], F32, name="sb_sb")
+        nc.sync.dma_start(sb_sb[:], sb.rearrange("(p t) o -> p (t o)", t=PACK))
+
+        def deal(name, words, words_dtype, per_col, plane, t0, t1, tag="", tag_s=""):
+            count = t1 - t0
+            dealt = keep.tile([P, count, P, per_col], words_dtype, name=name + "_words", align_bytes=64, tag=tag)
+            dealt_s = keep.tile([P, count, P], U8, name=name + "_scales", align_bytes=64, tag=tag_s)
+            nc.vector.tensor_copy(dealt_s[:], plane[:].rearrange("p (m t) -> p t m", t=PACK)[:, t0:t1, :])
+            nc.vector.tensor_copy(dealt[:], words[:].rearrange("p (m t b) -> p t m b", t=PACK, b=per_col)[:, t0:t1, :, :])
+            return [
+                (dealt[:, i, :, :].rearrange("p m b -> p (m b)"), dealt_s[:, i, :]) for i in range(count)
+            ]
+
+        xw = keep.tile([P, J], U32, name="xw", align_bytes=64)
+        xs = keep.tile([P, J], U8, name="xs", align_bytes=64)
+
+        def gather_tokens(lo, hi):
+            part = idx[:, lo // PER_COL : hi // PER_COL]
+            nc.vector.tensor_copy(xw[:, lo:hi], xw_all[:].bitcast(U32).indirect(part))
+
+        def product(weights, fmt, lo, hi, name, tag):
+            words, scales = weights
+            acc = psum.tile([P, hi - lo], F32, name="acc")
+            nc.tensor.matmul_mx(
+                out=acc[:], lhsT=words.bitcast(fmt), lhsT_scale=scales,
+                rhs=xw[:, lo:hi].bitcast(FP8X4), rhs_scale=xs[:, lo:hi], start=True, stop=True,
+            )
+            res = keep.tile([P, hi - lo], F32, name=name, tag=tag, align_bytes=64)
+            if name == "b_lo":
+                nc.scalar.activation(out=res[:], in_=acc[:], func=COPY)
+            else:
+                nc.vector.tensor_copy(res[:], acc[:])
+            return res
+
+        def scatter(board, places, lo, hi, values):
+            nc.scalar.activation(
+                out=board[:].indirect(places[:, lo // PER_COL : hi // PER_COL]), in_=values[:], func=COPY
+            )
+
+        spread_rows(w2s_all, w2s_staged)
+        w2d = deal("w2_first", w2w_all, U8, 2, w2s_all, 0, 1)
+        nc.vector.tensor_copy(xs[:], xs_all[:].indirect(idx[:]))
+        gather_tokens(0, HALF)
+        b_lo = product(w2d[0], FP4X4, 0, HALF, "b_lo", "b_lo")
+        scatter(boards["pv0"], idx3, 0, HALF, b_lo)
+        gather_tokens(HALF, J)
+        b_hi = product(w2d[0], FP4X4, HALF, J, "b_hi", "b_hi")
+        scatter(boards["pv0"], idx3, HALF, J, b_hi)
+        w2d = w2d + deal("w2_second", w2w_all, U8, 2, w2s_all, 1, 2, "xw_all", "xs_all")
+        b = [None] + [product(w2d[1], FP4X4, 0, J, "b1", "b1")]
+        scatter(boards["pv1"], idx3, 0, J, b[1])
+        spread_rows(ws_all, ws_staged)
+        wd = deal("w_first", ww_all, I32, 1, ws_all, 0, 1)
+        a = [product(wd[0], FP8X4, 0, J, "a0", "a0")]
+        wd = wd + deal("w_rest", ww_all, I32, 1, ws_all, 1, PACK)
+        a.append(product(wd[1], FP8X4, 0, J, "a1", "a1"))
+        w2d = w2d + deal("w2_rest", w2w_all, U8, 2, w2s_all, 2, PACK, "ww_all", "ws_all")
+        for t in range(2, PACK):
+            b.append(product(w2d[t], FP4X4, 0, J, "b%d" % t, "b%d" % t))
+            a.append(product(wd[t], FP8X4, 0, J, "a%d" % t, "last" if t == PACK - 1 else "a%d" % t))
+
+        ph, pl = [], []
+        for t in range(PACK):
+            pw, pv = boards["pw%d" % (t % 2)], boards["pv%d" % (t % 2)]
+            if t >= 2:
+                scatter(pv, idx3, 0, J, b[t])
+            scatter(pw, idx2, 0, J, a[t])
+            ph.append(keep.tile([P, C], F32, name="ph%d" % t))
+            pl.append(keep.tile([P, C], F32, name="pl%d" % t))
+            nc.vector.tensor_tensor(ph[t][:], pw[:], pv[:], MAX)
+            nc.vector.tensor_tensor(pl[t][:], pw[:], pv[:], MIN)
+
+        vsw = keep.tile([P, 2 * N], U8, name="vsw", align_bytes=64, tag="w2w_all")
+        vss = keep.tile([P, N], U8, name="vss", align_bytes=64, tag="w2s_all")
+        nc.vector.tensor_copy(vsw[:].bitcast(U16), vsw_all[:].indirect(idx6[:]))
+        nc.vector.tensor_copy(vss[:], vss_all[:].indirect(idx6[:]))
+
+        hid = keep.tile([P, 2, PACK, O], BF16, name="hid", tag="last", align_bytes=64)
+        out_rows = out.rearrange("(a p) d -> p a d", p=P)
+        for side, (board, places, weight) in enumerate(((ph, idx4, sa_sb), (pl, idx5, sb_sb))):
+            for t in range(PACK):
+                nc.scalar.activation(
+                    out=hid[:, side, t, :], in_=board[t][:].indirect(places[:]), func=COPY, scale=weight[:, t : t + 1]
+                )
+            woven = keep.tile([P, O, PACK], BF16, name="woven%d" % side, align_bytes=64)
+            nc.vector.tensor_copy(
+                woven[:].rearrange("p (c i) t -> p c t i", i=PACK),
+                hid[:, side, :, :].rearrange("p t (c i) -> p c t i", i=PACK),
+            )
+            codes = keep.tile([P, O], U32, name="codes%d" % side, align_bytes=64)
+            scales = keep.tile([P, O], U8, name="scales%d" % side, align_bytes=64)
+            nc.vector.quantize_mx(
+                out=codes[:].bitcast(FP8X4), scales=scales[:], in_=woven[:].rearrange("p d t -> p (d t)")
+            )
+            cols = slice(O * side, O * (side + 1))
+            operands = [
+                dict(
+                    lhsT=vsw[:, 2 * P * half : 2 * P * (half + 1)].bitcast(FP4X4),
+                    lhsT_scale=vss[:, P * half : P * (half + 1)],
+                    rhs=codes[:].bitcast(FP8X4), rhs_scale=scales[:], start=True, stop=True,
+                )
+                for half in range(N // P)
+            ]
+            if side == 0:
+                y_win = psum_out.tile([P, N // P, O], F32, name="y_win")
+                for half in range(N // P):
+                    nc.tensor.matmul_mx(out=y_win[:, half, :], **operands[half])
+            else:
+                res_win = keep.tile([P, N // P, O], F32, name="res_win")
+                nc.scalar.copy(res_win[:], y_win[:])
+                nc.scalar.dma_start(out_rows[:, :, 0:O], res_win[:])
+                for half in range(N // P):
+                    acc = psum_out.tile([P, O], F32, name="y_lose%d" % half)
+                    nc.tensor.matmul_mx(out=acc[:], **operands[half])
+                    res = keep.tile([P, O], F32, name="res_lose%d" % half)
+                    if half == 1:
+                        nc.scalar.copy(res[:], acc[:])
+                        nc.scalar.dma_start(out_rows[:, half, cols], res[:])
+                    else:
+                        nc.vector.tensor_copy(res[:], acc[:])
+                        nc.sync.dma_start(out_rows[:, half, cols], res[:])

@@ -32,6 +32,7 @@ def tile_picked_tokens_plain_twin_winnersides_store_plain_kernel(
     with ExitStack() as ctx:
         lists = ctx.enter_context(tc.tile_pool(name="lists", bufs=1))
         keep = ctx.enter_context(tc.tile_pool(name="keep", bufs=1))
+        placed = ctx.enter_context(tc.tile_pool(name="placed", bufs=1))
         psum = ctx.enter_context(tc.psum_pool(name="psum", bufs=4))
         psum_out = ctx.enter_context(tc.psum_pool(name="psum_out", bufs=1))
 
@@ -40,90 +41,70 @@ def tile_picked_tokens_plain_twin_winnersides_store_plain_kernel(
             nc.sync.dma_start(tile[:], src)
             return tile
 
-        def zeroed_plane(width, name, tag=""):
-            plane = keep.tile([P, width], U8, name=name, align_bytes=64, tag=tag)
-            nc.vector.memset(plane[:].bitcast(I32), 0)
-            return plane
-
         def load_plane_rows(queue, plane, scales, quads):
             rows = scales[0].bitcast(I32)
             for q in quads:
                 queue.dma_start(plane[QUAD * q : QUAD * q + PACK, :].bitcast(I32), rows[PACK * q : PACK * (q + 1), :])
 
-        def load_staged_rows(queue, scales, name):
-            staged = keep.tile([PACK, P // QUAD, R // 4], I32, name=name)
-            queue.dma_start(staged[:], scales[0].bitcast(I32).rearrange("(q i) c -> i q c", i=PACK))
-            return staged
-
-        def spread_rows(plane, staged):
-            for q in range(P // QUAD):
-                nc.vector.tensor_copy(plane[QUAD * q : QUAD * q + PACK, :].bitcast(I32), staged[:, q, :])
-
-        xs_all = zeroed_plane(T, "xs_all", "xs_all")
-        w2s_all = zeroed_plane(R, "w2s_all", "w2s_all")
-
-        ws_all = zeroed_plane(R, "ws_all", "ws_all")
+        xs_all = keep.tile([P, T], U8, name="xs_all")
+        w2s_all = keep.tile([P, R], U8, name="w2s_all")
+        ws_all = keep.tile([P, R], U8, name="ws_all")
+        vss_all = keep.tile([P, S], U8, name="vss_all")
+        for plane in (xs_all, w2s_all):
+            nc.vector.memset(plane[:].bitcast(I32), 0)
 
         idx = load_list(offs, "idx")
-        w2s_staged = load_staged_rows(nc.scalar, w2_scales, "w2s_staged")
+        w2s_staged = keep.tile([PACK, P // QUAD, R // 4], I32, name="w2s_staged")
+        nc.scalar.dma_start(w2s_staged[:], w2_scales[0].bitcast(I32).rearrange("(q i) c -> i q c", i=PACK))
         load_plane_rows(nc.scalar, xs_all, xt_scales, (1, 2, 3))
-        w2w_all = keep.tile([P, 2 * R], U8, name="w2w_all", align_bytes=64, tag="w2w_all")
+        w2w_all = keep.tile([P, R], U16, name="w2w_all")
         nc.sync.dma_start(w2w_all[:].bitcast(I32), w2_words[0].bitcast(I32))
         load_plane_rows(nc.sync, xs_all, xt_scales, (0,))
-        xw_all = keep.tile([P, T], I32, name="xw_all", align_bytes=64, tag="xw_all")
+        xw_all = placed.tile([P, T], I32, name="xw_all", align_bytes=64, offset=0)
         nc.sync.dma_start(xw_all[:], xt_words[0].rearrange("p c t -> p (c t)").bitcast(I32))
         idx3 = load_list(offs3, "idx3")
-        ws_staged = load_staged_rows(nc.sync, w_scales, "ws_staged")
-        ww_all = keep.tile([P, R], I32, name="ww_all", align_bytes=64, tag="ww_all")
-        nc.sync.dma_start(ww_all[:], w_words[0].rearrange("p c t -> p (c t)").bitcast(I32))
-        idx2 = load_list(offs2, "idx2")
-
-        boards = {}
-        for name in ("pv0", "pv1", "pw0", "pw1"):
-            boards[name] = keep.tile([P, C], F32, name=name)
-            nc.vector.memset(boards[name][:], 0.0)
-
-        vss_all = zeroed_plane(S, "vss_all")
         idx6 = load_list(offs6, "idx6")
+        ww_all = keep.tile([P, R], I32, name="ww_all")
+        nc.sync.dma_start(ww_all[:], w_words[0].rearrange("p c t -> p (c t)").bitcast(I32))
         vsw_all = keep.tile([P, S], U16, name="vsw_all")
         nc.sync.dma_start(vsw_all[:].bitcast(I32), vs_words[0].bitcast(I32))
-        load_plane_rows(nc.sync, vss_all, vs_scales, range(P // QUAD))
+
+        def zeroed_board(pool, name, **place):
+            board = pool.tile([P, C], F32, name=name, align_bytes=64, **place)
+            nc.vector.memset(board[:], 0.0)
+            return board
+
+        pv = [zeroed_board(keep, "pv%d" % t) for t in range(2)]
+        for plane, scales in ((ws_all, w_scales), (vss_all, vs_scales)):
+            nc.vector.memset(plane[:].bitcast(I32), 0)
+            load_plane_rows(nc.sync, plane, scales, range(P // QUAD))
         idx4 = load_list(offs4, "idx4")
         idx5 = load_list(offs5, "idx5")
         sa_sb = keep.tile([P, PACK], F32, name="sa_sb")
         nc.sync.dma_start(sa_sb[:], sa.rearrange("(p t) o -> p (t o)", t=PACK))
         sb_sb = keep.tile([P, PACK], F32, name="sb_sb")
         nc.sync.dma_start(sb_sb[:], sb.rearrange("(p t) o -> p (t o)", t=PACK))
+        idx2 = load_list(offs2, "idx2")
 
-        def deal(name, words, words_dtype, per_col, plane, t0, t1, tag="", tag_s=""):
-            count = t1 - t0
-            dealt = keep.tile([P, count, P, per_col], words_dtype, name=name + "_words", align_bytes=64, tag=tag)
-            dealt_s = keep.tile([P, count, P], U8, name=name + "_scales", align_bytes=64, tag=tag_s)
-            nc.vector.tensor_copy(dealt_s[:], plane[:].rearrange("p (m t) -> p t m", t=PACK)[:, t0:t1, :])
-            nc.vector.tensor_copy(dealt[:], words[:].rearrange("p (m t b) -> p t m b", t=PACK, b=per_col)[:, t0:t1, :, :])
-            return [
-                (dealt[:, i, :, :].rearrange("p m b -> p (m b)"), dealt_s[:, i, :]) for i in range(count)
-            ]
+        def by_tile(ap, t0, t1):
+            return ap.rearrange("p (m t) -> p t m", t=PACK)[:, t0:t1, :]
 
-        xw = keep.tile([P, J], U32, name="xw", align_bytes=64)
-        xs = keep.tile([P, J], U8, name="xs", align_bytes=64)
+        def gather(dst, window, lo, hi):
+            nc.vector.tensor_copy(dst, window.indirect(idx[:, lo // PER_COL : hi // PER_COL]))
 
-        def gather_tokens(lo, hi):
-            part = idx[:, lo // PER_COL : hi // PER_COL]
-            nc.vector.tensor_copy(xw[:, lo:hi], xw_all[:].bitcast(U32).indirect(part))
-
-        def product(weights, fmt, lo, hi, name, tag):
-            words, scales = weights
-            acc = psum.tile([P, hi - lo], F32, name="acc")
+        def multiply(acc, words, scales, fmt, half):
             nc.tensor.matmul_mx(
-                out=acc[:], lhsT=words.bitcast(fmt), lhsT_scale=scales,
-                rhs=xw[:, lo:hi].bitcast(FP8X4), rhs_scale=xs[:, lo:hi], start=True, stop=True,
+                out=acc, lhsT=words.bitcast(fmt), lhsT_scale=scales,
+                rhs=xw[:, HALF * half : HALF * (half + 1)].bitcast(FP8X4), rhs_scale=xs[half][:],
+                start=True, stop=True,
             )
-            res = keep.tile([P, hi - lo], F32, name=name, tag=tag, align_bytes=64)
-            if name == "b_lo":
-                nc.scalar.activation(out=res[:], in_=acc[:], func=COPY)
-            else:
-                nc.vector.tensor_copy(res[:], acc[:])
+
+        def product(words, scales, fmt, name, tag=""):
+            acc = psum.tile([P, J], F32, name="acc")
+            for half in range(2):
+                multiply(acc[:, HALF * half : HALF * (half + 1)], words, scales, fmt, half)
+            res = keep.tile([P, J], F32, name=name, tag=tag, align_bytes=64)
+            nc.vector.tensor_copy(res[:], acc[:])
             return res
 
         def scatter(board, places, lo, hi, values):
@@ -131,43 +112,67 @@ def tile_picked_tokens_plain_twin_winnersides_store_plain_kernel(
                 out=board[:].indirect(places[:, lo // PER_COL : hi // PER_COL]), in_=values[:], func=COPY
             )
 
-        spread_rows(w2s_all, w2s_staged)
-        w2d = deal("w2_first", w2w_all, U8, 2, w2s_all, 0, 1)
-        nc.vector.tensor_copy(xs[:], xs_all[:].indirect(idx[:]))
-        gather_tokens(0, HALF)
-        b_lo = product(w2d[0], FP4X4, 0, HALF, "b_lo", "b_lo")
-        scatter(boards["pv0"], idx3, 0, HALF, b_lo)
-        gather_tokens(HALF, J)
-        b_hi = product(w2d[0], FP4X4, HALF, J, "b_hi", "b_hi")
-        scatter(boards["pv0"], idx3, HALF, J, b_hi)
-        w2d = w2d + deal("w2_second", w2w_all, U8, 2, w2s_all, 1, 2, "xw_all", "xs_all")
-        b = [None] + [product(w2d[1], FP4X4, 0, J, "b1", "b1")]
-        scatter(boards["pv1"], idx3, 0, J, b[1])
-        spread_rows(ws_all, ws_staged)
-        wd = deal("w_first", ww_all, I32, 1, ws_all, 0, 1)
-        a = [product(wd[0], FP8X4, 0, J, "a0", "a0")]
-        wd = wd + deal("w_rest", ww_all, I32, 1, ws_all, 1, PACK)
-        a.append(product(wd[1], FP8X4, 0, J, "a1", "a1"))
-        w2d = w2d + deal("w2_rest", w2w_all, U8, 2, w2s_all, 2, PACK, "ww_all", "ws_all")
-        for t in range(2, PACK):
-            b.append(product(w2d[t], FP4X4, 0, J, "b%d" % t, "b%d" % t))
-            a.append(product(wd[t], FP8X4, 0, J, "a%d" % t, "last" if t == PACK - 1 else "a%d" % t))
+        for q in range(P // QUAD):
+            nc.vector.tensor_copy(w2s_all[QUAD * q : QUAD * q + PACK, :].bitcast(I32), w2s_staged[:, q, :])
+        w2s_0 = keep.tile([P, 1, P], U8, name="w2s_0", align_bytes=64)
+        nc.vector.tensor_copy(w2s_0[:], by_tile(w2s_all[:], 0, 1))
+        w2w_0 = keep.tile([P, 1, 2 * P], U8, name="w2w_0", align_bytes=64, tag="w2w_0")
+        nc.scalar.copy(w2w_0[:].bitcast(U16), by_tile(w2w_all[:], 0, 1))
+        w2w_rest = keep.tile([P, PACK - 1, 2 * P], U8, name="w2w_rest", align_bytes=64, tag="w2w_rest")
+        nc.scalar.copy(w2w_rest[:].bitcast(U16), by_tile(w2w_all[:], 1, PACK))
+
+        xw = keep.tile([P, J], U32, name="xw", align_bytes=64)
+        xs = [keep.tile([P, HALF], U8, name="xs_lo", align_bytes=64)]
+        gather(xs[0][:], xs_all[:], 0, HALF)
+        gather(xw[:, 0:HALF], xw_all[:].bitcast(U32), 0, HALF)
+        acc_lo = psum.tile([P, HALF], F32, name="acc")
+        multiply(acc_lo[:], w2w_0[:, 0, :], w2s_0[:, 0, :], FP4X4, 0)
+        b_lo = keep.tile([P, HALF], F32, name="b_lo")
+        nc.scalar.activation(out=b_lo[:], in_=acc_lo[:], func=COPY)
+        scatter(pv[0], idx3, 0, HALF, b_lo)
+
+        gather(xw[:, HALF:J], xw_all[:].bitcast(U32), HALF, J)
+        xs.append(placed.tile([P, HALF], U8, name="xs_hi", align_bytes=64, offset=0))
+        gather(xs[1][:], xs_all[:], HALF, J)
+        acc_hi = psum.tile([P, HALF], F32, name="acc")
+        multiply(acc_hi[:], w2w_0[:, 0, :], w2s_0[:, 0, :], FP4X4, 1)
+        b_hi = keep.tile([P, HALF], F32, name="b_hi")
+        nc.vector.tensor_copy(b_hi[:], acc_hi[:])
+        scatter(pv[0], idx3, HALF, J, b_hi)
+
+        w2s_1 = placed.tile([P, 1, P], U8, name="w2s_1", align_bytes=64, offset=3968)
+        nc.vector.tensor_copy(w2s_1[:], by_tile(w2s_all[:], 1, 2))
+        w2s_rest = placed.tile([P, 2, P], U8, name="w2s_rest", align_bytes=64, offset=128)
+        nc.vector.tensor_copy(w2s_rest[:], by_tile(w2s_all[:], 2, PACK))
+        scatter(pv[1], idx3, 0, J, product(w2w_rest[:, 0, :], w2s_1[:, 0, :], FP4X4, "b1"))
+        b = [product(w2w_rest[:, t - 1, :], w2s_rest[:, t - 2, :], FP4X4, "b%d" % t) for t in (2, 3)]
+        pv.append(zeroed_board(keep, "pv2", tag="w2w_0"))
+        pv.append(zeroed_board(placed, "pv3", offset=3968))
+        for t in (2, 3):
+            scatter(pv[t], idx3, 0, J, b[t - 2])
+
+        ws_dealt = keep.tile([P, PACK, P], U8, name="ws_dealt", align_bytes=64)
+        nc.vector.tensor_copy(ws_dealt[:], by_tile(ws_all[:], 0, PACK))
+        ww_dealt = keep.tile([P, PACK, P], I32, name="ww_dealt", align_bytes=64)
+        nc.vector.tensor_copy(ww_dealt[:], by_tile(ww_all[:], 0, PACK))
+        a = [
+            product(ww_dealt[:, t, :], ws_dealt[:, t, :], FP8X4, "a%d" % t, "last" if t == PACK - 1 else "")
+            for t in range(PACK)
+        ]
+        pw = [zeroed_board(keep, "pw0", tag="w2w_rest"), zeroed_board(placed, "pw1", offset=128)]
+
+        vsw = keep.tile([P, 2 * N], U8, name="vsw", align_bytes=64)
+        vss = keep.tile([P, N], U8, name="vss", align_bytes=64)
+        nc.vector.tensor_copy(vsw[:].bitcast(U16), vsw_all[:].indirect(idx6[:]))
+        nc.vector.tensor_copy(vss[:], vss_all[:].indirect(idx6[:]))
 
         ph, pl = [], []
         for t in range(PACK):
-            pw, pv = boards["pw%d" % (t % 2)], boards["pv%d" % (t % 2)]
-            if t >= 2:
-                scatter(pv, idx3, 0, J, b[t])
-            scatter(pw, idx2, 0, J, a[t])
+            scatter(pw[t % 2], idx2, 0, J, a[t])
             ph.append(keep.tile([P, C], F32, name="ph%d" % t))
             pl.append(keep.tile([P, C], F32, name="pl%d" % t))
-            nc.vector.tensor_tensor(ph[t][:], pw[:], pv[:], MAX)
-            nc.vector.tensor_tensor(pl[t][:], pw[:], pv[:], MIN)
-
-        vsw = keep.tile([P, 2 * N], U8, name="vsw", align_bytes=64, tag="w2w_all")
-        vss = keep.tile([P, N], U8, name="vss", align_bytes=64, tag="w2s_all")
-        nc.vector.tensor_copy(vsw[:].bitcast(U16), vsw_all[:].indirect(idx6[:]))
-        nc.vector.tensor_copy(vss[:], vss_all[:].indirect(idx6[:]))
+            nc.vector.tensor_tensor(ph[t][:], pw[t % 2][:], pv[t][:], MAX)
+            nc.vector.tensor_tensor(pl[t][:], pw[t % 2][:], pv[t][:], MIN)
 
         hid = keep.tile([P, 2, PACK, O], BF16, name="hid", tag="last", align_bytes=64)
         out_rows = out.rearrange("(a p) d -> p a d", p=P)
@@ -177,10 +182,11 @@ def tile_picked_tokens_plain_twin_winnersides_store_plain_kernel(
                     out=hid[:, side, t, :], in_=board[t][:].indirect(places[:]), func=COPY, scale=weight[:, t : t + 1]
                 )
             woven = keep.tile([P, O, PACK], BF16, name="woven%d" % side, align_bytes=64)
-            nc.vector.tensor_copy(
-                woven[:].rearrange("p (c i) t -> p c t i", i=PACK),
-                hid[:, side, :, :].rearrange("p t (c i) -> p c t i", i=PACK),
-            )
+            for t0 in (0, 2):
+                nc.vector.tensor_copy(
+                    woven[:, :, t0 : t0 + 2].rearrange("p (c i) t -> p c t i", i=PACK),
+                    hid[:, side, t0 : t0 + 2, :].rearrange("p t (c i) -> p c t i", i=PACK),
+                )
             codes = keep.tile([P, O], U32, name="codes%d" % side, align_bytes=64)
             scales = keep.tile([P, O], U8, name="scales%d" % side, align_bytes=64)
             nc.vector.quantize_mx(

@@ -46,7 +46,7 @@ def tile_picked_tokens_plain_twin_winnersides_store_plain_kernel(
             for q in quads:
                 queue.dma_start(plane[QUAD * q : QUAD * q + PACK, :].bitcast(I32), rows[PACK * q : PACK * (q + 1), :])
 
-        xs_all = keep.tile([P, T], U8, name="xs_all")
+        xs_all = keep.tile([P, T], U8, name="xs_all", align_bytes=64, tag="xs_all")
         w2s_all = keep.tile([P, R], U8, name="w2s_all")
         ws_all = keep.tile([P, R], U8, name="ws_all")
         vss_all = keep.tile([P, S], U8, name="vss_all")
@@ -54,14 +54,13 @@ def tile_picked_tokens_plain_twin_winnersides_store_plain_kernel(
             nc.vector.memset(plane[:].bitcast(I32), 0)
 
         idx = load_list(offs, "idx")
-        w2s_staged = keep.tile([PACK, P // QUAD, R // 4], I32, name="w2s_staged")
-        nc.scalar.dma_start(w2s_staged[:], w2_scales[0].bitcast(I32).rearrange("(q i) c -> i q c", i=PACK))
-        load_plane_rows(nc.scalar, xs_all, xt_scales, (1, 2, 3))
-        w2w_all = keep.tile([P, R], U16, name="w2w_all")
-        nc.sync.dma_start(w2w_all[:].bitcast(I32), w2_words[0].bitcast(I32))
-        load_plane_rows(nc.sync, xs_all, xt_scales, (0,))
         xw_all = placed.tile([P, T], I32, name="xw_all", align_bytes=64, offset=0)
         nc.sync.dma_start(xw_all[:], xt_words[0].rearrange("p c t -> p (c t)").bitcast(I32))
+        w2s_staged = keep.tile([PACK, P // QUAD, R // 4], I32, name="w2s_staged")
+        nc.scalar.dma_start(w2s_staged[:], w2_scales[0].bitcast(I32).rearrange("(q i) c -> i q c", i=PACK))
+        load_plane_rows(nc.scalar, xs_all, xt_scales, range(P // QUAD))
+        w2w_all = keep.tile([P, R], U16, name="w2w_all")
+        nc.sync.dma_start(w2w_all[:].bitcast(I32), w2_words[0].bitcast(I32))
         idx3 = load_list(offs3, "idx3")
         idx6 = load_list(offs6, "idx6")
         ww_all = keep.tile([P, R], I32, name="ww_all")
@@ -95,7 +94,7 @@ def tile_picked_tokens_plain_twin_winnersides_store_plain_kernel(
         def multiply(acc, words, scales, fmt, half):
             nc.tensor.matmul_mx(
                 out=acc, lhsT=words.bitcast(fmt), lhsT_scale=scales,
-                rhs=xw[:, HALF * half : HALF * (half + 1)].bitcast(FP8X4), rhs_scale=xs[half][:],
+                rhs=xw[half][:].bitcast(FP8X4), rhs_scale=xs[:, HALF * half : HALF * (half + 1)],
                 start=True, stop=True,
             )
 
@@ -113,27 +112,28 @@ def tile_picked_tokens_plain_twin_winnersides_store_plain_kernel(
             )
 
         for q in range(P // QUAD):
-            nc.vector.tensor_copy(w2s_all[QUAD * q : QUAD * q + PACK, :].bitcast(I32), w2s_staged[:, q, :])
+            engine = nc.gpsimd if q == 0 else nc.vector
+            engine.tensor_copy(w2s_all[QUAD * q : QUAD * q + PACK, :].bitcast(I32), w2s_staged[:, q, :])
         w2s_0 = keep.tile([P, 1, P], U8, name="w2s_0", align_bytes=64)
-        nc.vector.tensor_copy(w2s_0[:], by_tile(w2s_all[:], 0, 1))
+        nc.gpsimd.tensor_copy(w2s_0[:], by_tile(w2s_all[:], 0, 1))
         w2w_0 = keep.tile([P, 1, 2 * P], U8, name="w2w_0", align_bytes=64, tag="w2w_0")
         nc.scalar.copy(w2w_0[:].bitcast(U16), by_tile(w2w_all[:], 0, 1))
         w2w_rest = keep.tile([P, PACK - 1, 2 * P], U8, name="w2w_rest", align_bytes=64, tag="w2w_rest")
         nc.scalar.copy(w2w_rest[:].bitcast(U16), by_tile(w2w_all[:], 1, PACK))
 
-        xw = keep.tile([P, J], U32, name="xw", align_bytes=64)
-        xs = [keep.tile([P, HALF], U8, name="xs_lo", align_bytes=64)]
-        gather(xs[0][:], xs_all[:], 0, HALF)
-        gather(xw[:, 0:HALF], xw_all[:].bitcast(U32), 0, HALF)
+        xw = [keep.tile([P, HALF], U32, name="xw_lo", align_bytes=64)]
+        xs = keep.tile([P, J], U8, name="xs", align_bytes=64)
+        gather(xw[0][:], xw_all[:].bitcast(U32), 0, HALF)
+        gather(xs[:, 0:HALF], xs_all[:], 0, HALF)
         acc_lo = psum.tile([P, HALF], F32, name="acc")
         multiply(acc_lo[:], w2w_0[:, 0, :], w2s_0[:, 0, :], FP4X4, 0)
         b_lo = keep.tile([P, HALF], F32, name="b_lo")
         nc.scalar.activation(out=b_lo[:], in_=acc_lo[:], func=COPY)
         scatter(pv[0], idx3, 0, HALF, b_lo)
 
-        gather(xw[:, HALF:J], xw_all[:].bitcast(U32), HALF, J)
-        xs.append(placed.tile([P, HALF], U8, name="xs_hi", align_bytes=64, offset=0))
-        gather(xs[1][:], xs_all[:], HALF, J)
+        gather(xs[:, HALF:J], xs_all[:], HALF, J)
+        xw.append(keep.tile([P, HALF], U32, name="xw_hi", align_bytes=64, tag="xs_all"))
+        gather(xw[1][:], xw_all[:].bitcast(U32), HALF, J)
         acc_hi = psum.tile([P, HALF], F32, name="acc")
         multiply(acc_hi[:], w2w_0[:, 0, :], w2s_0[:, 0, :], FP4X4, 1)
         b_hi = keep.tile([P, HALF], F32, name="b_hi")
@@ -151,9 +151,9 @@ def tile_picked_tokens_plain_twin_winnersides_store_plain_kernel(
         for t in (2, 3):
             scatter(pv[t], idx3, 0, J, b[t - 2])
 
-        ws_dealt = keep.tile([P, PACK, P], U8, name="ws_dealt", align_bytes=64)
+        ws_dealt = keep.tile([P, PACK, P], U8, name="ws_dealt", align_bytes=64, tag="ws_dealt")
         nc.vector.tensor_copy(ws_dealt[:], by_tile(ws_all[:], 0, PACK))
-        ww_dealt = keep.tile([P, PACK, P], I32, name="ww_dealt", align_bytes=64)
+        ww_dealt = keep.tile([P, PACK, P], I32, name="ww_dealt", align_bytes=64, tag="ww_dealt")
         nc.vector.tensor_copy(ww_dealt[:], by_tile(ww_all[:], 0, PACK))
         a = [
             product(ww_dealt[:, t, :], ws_dealt[:, t, :], FP8X4, "a%d" % t, "last" if t == PACK - 1 else "")
@@ -161,8 +161,8 @@ def tile_picked_tokens_plain_twin_winnersides_store_plain_kernel(
         ]
         pw = [zeroed_board(keep, "pw0", tag="w2w_rest"), zeroed_board(placed, "pw1", offset=128)]
 
-        vsw = keep.tile([P, 2 * N], U8, name="vsw", align_bytes=64)
-        vss = keep.tile([P, N], U8, name="vss", align_bytes=64)
+        vsw = keep.tile([P, 2 * N], U8, name="vsw", align_bytes=64, tag="ww_dealt")
+        vss = keep.tile([P, N], U8, name="vss", align_bytes=64, tag="ws_dealt")
         nc.vector.tensor_copy(vsw[:].bitcast(U16), vsw_all[:].indirect(idx6[:]))
         nc.vector.tensor_copy(vss[:], vss_all[:].indirect(idx6[:]))
 

@@ -2,7 +2,7 @@ from contextlib import ExitStack
 
 import concourse.mybir as mybir
 
-K, J, R, T, C, O, U, D, N, S = 512, 256, 512, 1024, 512, 128, 128, 256, 256, 1024
+K, J, R, T, C, O, D, N, S = 512, 256, 512, 1024, 512, 128, 256, 256, 1024
 FLOPS = 2 * K * R * J * 2 + 2 * R * N * D
 
 F32 = mybir.dt.float32
@@ -20,8 +20,18 @@ MIN = mybir.AluOpType.min
 P = 128
 PACK = 4
 QUAD = 32
+QUADS = P // QUAD
 HALF = J // 2
 PER_COL = 16
+ALIGN = 64
+PW_BOARDS = 3
+
+BOARD_BYTES = 4 * C
+AT_XW_ALL = 0
+AT_W2S_REST = 0
+AT_W2S_1 = 4 * T - P
+AT_WW_DEALT = AT_W2S_1 + BOARD_BYTES
+AT_PW_2 = AT_WW_DEALT + 2 * N
 
 
 def tile_picked_tokens_plain_twin_winnersides_store_plain_kernel(
@@ -37,16 +47,27 @@ def tile_picked_tokens_plain_twin_winnersides_store_plain_kernel(
         psum_out = ctx.enter_context(tc.psum_pool(name="psum_out", bufs=1))
 
         def load_list(src, name):
-            tile = lists.tile(list(src.shape), U16, name=name)
-            nc.sync.dma_start(tile[:], src)
-            return tile
+            offsets = lists.tile(list(src.shape), U16, name=name)
+            nc.sync.dma_start(offsets[:], src)
+            return offsets
 
-        def load_plane_rows(queue, plane, scales, quads):
+        def live_rows(plane, q):
+            return plane[QUAD * q : QUAD * q + PACK, :].bitcast(I32)
+
+        def load_plane(queue, plane, scales):
             rows = scales[0].bitcast(I32)
-            for q in quads:
-                queue.dma_start(plane[QUAD * q : QUAD * q + PACK, :].bitcast(I32), rows[PACK * q : PACK * (q + 1), :])
+            for q in range(QUADS):
+                queue.dma_start(live_rows(plane, q), rows[PACK * q : PACK * (q + 1), :])
 
-        xs_all = keep.tile([P, T], U8, name="xs_all", align_bytes=64, tag="xs_all")
+        def zeroed_board(pool, name, **place):
+            board = pool.tile([P, C], F32, name=name, align_bytes=ALIGN, **place)
+            nc.vector.memset(board[:], 0.0)
+            return board
+
+        def by_tile(matrix, t0, t1):
+            return matrix.rearrange("p (m t) -> p t m", t=PACK)[:, t0:t1, :]
+
+        xs_all = keep.tile([P, T], U8, name="xs_all", align_bytes=ALIGN, tag="xs_all")
         w2s_all = keep.tile([P, R], U8, name="w2s_all")
         ws_all = keep.tile([P, R], U8, name="ws_all")
         vss_all = keep.tile([P, S], U8, name="vss_all")
@@ -54,42 +75,35 @@ def tile_picked_tokens_plain_twin_winnersides_store_plain_kernel(
             nc.vector.memset(plane[:].bitcast(I32), 0)
 
         idx = load_list(offs, "idx")
-        xw_all = placed.tile([P, T], I32, name="xw_all", align_bytes=64, offset=0)
+        xw_all = placed.tile([P, T], I32, name="xw_all", align_bytes=ALIGN, offset=AT_XW_ALL)
         nc.sync.dma_start(xw_all[:], xt_words[0].rearrange("p c t -> p (c t)").bitcast(I32))
-        w2s_staged = keep.tile([PACK, P // QUAD, R // 4], I32, name="w2s_staged")
+        w2s_staged = keep.tile([PACK, QUADS, R // 4], I32, name="w2s_staged")
         nc.scalar.dma_start(w2s_staged[:], w2_scales[0].bitcast(I32).rearrange("(q i) c -> i q c", i=PACK))
-        load_plane_rows(nc.scalar, xs_all, xt_scales, range(P // QUAD))
+        load_plane(nc.scalar, xs_all, xt_scales)
         w2w_all = keep.tile([P, R], U16, name="w2w_all")
         nc.sync.dma_start(w2w_all[:].bitcast(I32), w2_words[0].bitcast(I32))
+
         idx3 = load_list(offs3, "idx3")
         idx6 = load_list(offs6, "idx6")
         ww_all = keep.tile([P, R], I32, name="ww_all")
         nc.sync.dma_start(ww_all[:], w_words[0].rearrange("p c t -> p (c t)").bitcast(I32))
         vsw_all = keep.tile([P, S], U16, name="vsw_all")
         nc.sync.dma_start(vsw_all[:].bitcast(I32), vs_words[0].bitcast(I32))
-
-        def zeroed_board(pool, name, **place):
-            board = pool.tile([P, C], F32, name=name, align_bytes=64, **place)
-            nc.vector.memset(board[:], 0.0)
-            return board
-
         pv = [zeroed_board(keep, "pv%d" % t) for t in range(2)]
         for plane, scales in ((ws_all, w_scales), (vss_all, vs_scales)):
             nc.vector.memset(plane[:].bitcast(I32), 0)
-            load_plane_rows(nc.sync, plane, scales, range(P // QUAD))
+            load_plane(nc.sync, plane, scales)
         idx4 = load_list(offs4, "idx4")
         idx5 = load_list(offs5, "idx5")
-        sa_sb = keep.tile([P, PACK], F32, name="sa_sb")
-        nc.sync.dma_start(sa_sb[:], sa.rearrange("(p t) o -> p (t o)", t=PACK))
-        sb_sb = keep.tile([P, PACK], F32, name="sb_sb")
-        nc.sync.dma_start(sb_sb[:], sb.rearrange("(p t) o -> p (t o)", t=PACK))
+        sa_tiles = keep.tile([P, PACK], F32, name="sa_tiles")
+        nc.sync.dma_start(sa_tiles[:], sa.rearrange("(p t) o -> p (t o)", t=PACK))
+        sb_tiles = keep.tile([P, PACK], F32, name="sb_tiles")
+        nc.sync.dma_start(sb_tiles[:], sb.rearrange("(p t) o -> p (t o)", t=PACK))
         idx2 = load_list(offs2, "idx2")
 
-        def by_tile(ap, t0, t1):
-            return ap.rearrange("p (m t) -> p t m", t=PACK)[:, t0:t1, :]
-
-        def gather(dst, window, lo, hi):
-            nc.vector.tensor_copy(dst, window.indirect(idx[:, lo // PER_COL : hi // PER_COL]))
+        def gather_slots(dst, window, half):
+            cols = HALF // PER_COL
+            nc.vector.tensor_copy(dst, window.indirect(idx[:, cols * half : cols * (half + 1)]))
 
         def multiply(acc, words, scales, fmt, half):
             nc.tensor.matmul_mx(
@@ -102,120 +116,121 @@ def tile_picked_tokens_plain_twin_winnersides_store_plain_kernel(
             acc = psum.tile([P, J], F32, name="acc")
             for half in range(2):
                 multiply(acc[:, HALF * half : HALF * (half + 1)], words, scales, fmt, half)
-            res = keep.tile([P, J], F32, name=name, tag=tag, align_bytes=64)
-            nc.vector.tensor_copy(res[:], acc[:])
-            return res
+            values = keep.tile([P, J], F32, name=name, tag=tag, align_bytes=ALIGN)
+            nc.vector.tensor_copy(values[:], acc[:])
+            return values
 
-        def scatter(board, places, lo, hi, values):
-            nc.scalar.activation(
-                out=board[:].indirect(places[:, lo // PER_COL : hi // PER_COL]), in_=values[:], func=COPY
-            )
+        def scatter(board, offsets, values):
+            nc.scalar.activation(out=board[:].indirect(offsets), in_=values[:], func=COPY)
 
-        for q in range(P // QUAD):
-            engine = nc.gpsimd if q == 0 else nc.vector
-            engine.tensor_copy(w2s_all[QUAD * q : QUAD * q + PACK, :].bitcast(I32), w2s_staged[:, q, :])
-        w2s_0 = keep.tile([P, 1, P], U8, name="w2s_0", align_bytes=64)
-        nc.gpsimd.tensor_copy(w2s_0[:], by_tile(w2s_all[:], 0, 1))
-        w2w_0 = keep.tile([P, 1, 2 * P], U8, name="w2w_0", align_bytes=64, tag="w2w_0")
+        for q in range(QUADS):
+            nc.vector.tensor_copy(live_rows(w2s_all, q), w2s_staged[:, q, :])
+        w2s_0 = keep.tile([P, 1, P], U8, name="w2s_0", align_bytes=ALIGN)
+        nc.vector.tensor_copy(w2s_0[:], by_tile(w2s_all[:], 0, 1))
+        w2w_0 = keep.tile([P, 1, 2 * P], U8, name="w2w_0", align_bytes=ALIGN, tag="w2w_0")
         nc.scalar.copy(w2w_0[:].bitcast(U16), by_tile(w2w_all[:], 0, 1))
-        w2w_rest = keep.tile([P, PACK - 1, 2 * P], U8, name="w2w_rest", align_bytes=64, tag="w2w_rest")
+        w2w_rest = keep.tile([P, PACK - 1, 2 * P], U8, name="w2w_rest", align_bytes=ALIGN, tag="w2w_rest")
         nc.scalar.copy(w2w_rest[:].bitcast(U16), by_tile(w2w_all[:], 1, PACK))
 
-        xw = [keep.tile([P, HALF], U32, name="xw_lo", align_bytes=64)]
-        xs = keep.tile([P, J], U8, name="xs", align_bytes=64)
-        gather(xw[0][:], xw_all[:].bitcast(U32), 0, HALF)
-        gather(xs[:, 0:HALF], xs_all[:], 0, HALF)
+        xw = [keep.tile([P, HALF], U32, name="xw_lo", align_bytes=ALIGN)]
+        xs = keep.tile([P, J], U8, name="xs", align_bytes=ALIGN)
+        gather_slots(xw[0][:], xw_all[:].bitcast(U32), 0)
+        gather_slots(xs[:, 0:HALF], xs_all[:], 0)
         acc_lo = psum.tile([P, HALF], F32, name="acc")
         multiply(acc_lo[:], w2w_0[:, 0, :], w2s_0[:, 0, :], FP4X4, 0)
-        b_lo = keep.tile([P, HALF], F32, name="b_lo")
-        nc.scalar.activation(out=b_lo[:], in_=acc_lo[:], func=COPY)
-        scatter(pv[0], idx3, 0, HALF, b_lo)
+        b0_lo = keep.tile([P, HALF], F32, name="b0_lo")
+        nc.scalar.activation(out=b0_lo[:], in_=acc_lo[:], func=COPY)
+        scatter(pv[0], idx3[:, 0 : HALF // PER_COL], b0_lo)
 
-        gather(xs[:, HALF:J], xs_all[:], HALF, J)
-        xw.append(keep.tile([P, HALF], U32, name="xw_hi", align_bytes=64, tag="xs_all"))
-        gather(xw[1][:], xw_all[:].bitcast(U32), HALF, J)
+        gather_slots(xs[:, HALF:J], xs_all[:], 1)
+        xw.append(keep.tile([P, HALF], U32, name="xw_hi", align_bytes=ALIGN, tag="xs_all"))
+        gather_slots(xw[1][:], xw_all[:].bitcast(U32), 1)
         acc_hi = psum.tile([P, HALF], F32, name="acc")
         multiply(acc_hi[:], w2w_0[:, 0, :], w2s_0[:, 0, :], FP4X4, 1)
-        b_hi = keep.tile([P, HALF], F32, name="b_hi")
-        nc.vector.tensor_copy(b_hi[:], acc_hi[:])
-        scatter(pv[0], idx3, HALF, J, b_hi)
+        b0_hi = keep.tile([P, HALF], F32, name="b0_hi")
+        nc.vector.tensor_copy(b0_hi[:], acc_hi[:])
+        scatter(pv[0], idx3[:, HALF // PER_COL : J // PER_COL], b0_hi)
 
-        w2s_1 = placed.tile([P, 1, P], U8, name="w2s_1", align_bytes=64, offset=3968)
+        w2s_1 = placed.tile([P, 1, P], U8, name="w2s_1", align_bytes=ALIGN, offset=AT_W2S_1)
         nc.vector.tensor_copy(w2s_1[:], by_tile(w2s_all[:], 1, 2))
-        w2s_rest = placed.tile([P, 2, P], U8, name="w2s_rest", align_bytes=64, offset=128)
+        w2s_rest = placed.tile([P, 2, P], U8, name="w2s_rest", align_bytes=ALIGN, offset=AT_W2S_REST)
         nc.vector.tensor_copy(w2s_rest[:], by_tile(w2s_all[:], 2, PACK))
-        scatter(pv[1], idx3, 0, J, product(w2w_rest[:, 0, :], w2s_1[:, 0, :], FP4X4, "b1"))
-        b = [product(w2w_rest[:, t - 1, :], w2s_rest[:, t - 2, :], FP4X4, "b%d" % t) for t in (2, 3)]
+        scatter(pv[1], idx3[:], product(w2w_rest[:, 0, :], w2s_1[:, 0, :], FP4X4, "b1"))
+        b_late = [product(w2w_rest[:, t - 1, :], w2s_rest[:, t - 2, :], FP4X4, "b%d" % t) for t in (2, 3)]
         pv.append(zeroed_board(keep, "pv2", tag="w2w_0"))
-        pv.append(zeroed_board(placed, "pv3", offset=3968))
+        pv.append(zeroed_board(placed, "pv3", offset=AT_W2S_1))
         for t in (2, 3):
-            scatter(pv[t], idx3, 0, J, b[t - 2])
+            scatter(pv[t], idx3[:], b_late[t - 2])
 
-        ws_dealt = keep.tile([P, PACK, P], U8, name="ws_dealt", align_bytes=64, tag="ws_dealt")
+        ws_dealt = keep.tile([P, PACK, P], U8, name="ws_dealt", align_bytes=ALIGN, tag="ws_dealt")
         nc.vector.tensor_copy(ws_dealt[:], by_tile(ws_all[:], 0, PACK))
-        ww_dealt = keep.tile([P, PACK, P], I32, name="ww_dealt", align_bytes=64, tag="ww_dealt")
+        ww_dealt = placed.tile([P, PACK, P], I32, name="ww_dealt", align_bytes=ALIGN, offset=AT_WW_DEALT)
         nc.vector.tensor_copy(ww_dealt[:], by_tile(ww_all[:], 0, PACK))
         a = [
-            product(ww_dealt[:, t, :], ws_dealt[:, t, :], FP8X4, "a%d" % t, "last" if t == PACK - 1 else "")
+            product(ww_dealt[:, t, :], ws_dealt[:, t, :], FP8X4, "a%d" % t, "last_values" if t == PACK - 1 else "")
             for t in range(PACK)
         ]
-        pw = [zeroed_board(keep, "pw0", tag="w2w_rest"), zeroed_board(placed, "pw1", offset=128)]
+        pw = [
+            zeroed_board(keep, "pw0", tag="w2w_rest"),
+            zeroed_board(placed, "pw1", offset=AT_W2S_REST),
+            zeroed_board(placed, "pw2", offset=AT_PW_2),
+        ]
 
-        vsw = keep.tile([P, 2 * N], U8, name="vsw", align_bytes=64, tag="ww_dealt")
-        vss = keep.tile([P, N], U8, name="vss", align_bytes=64, tag="ws_dealt")
+        vsw = placed.tile([P, 2 * N], U8, name="vsw", align_bytes=ALIGN, offset=AT_WW_DEALT)
+        vss = keep.tile([P, N], U8, name="vss", align_bytes=ALIGN, tag="ws_dealt")
         nc.vector.tensor_copy(vsw[:].bitcast(U16), vsw_all[:].indirect(idx6[:]))
         nc.vector.tensor_copy(vss[:], vss_all[:].indirect(idx6[:]))
 
         ph, pl = [], []
         for t in range(PACK):
-            scatter(pw[t % 2], idx2, 0, J, a[t])
+            board_a = pw[t % PW_BOARDS]
+            scatter(board_a, idx2[:], a[t])
             ph.append(keep.tile([P, C], F32, name="ph%d" % t))
             pl.append(keep.tile([P, C], F32, name="pl%d" % t))
-            nc.vector.tensor_tensor(ph[t][:], pw[t % 2][:], pv[t][:], MAX)
-            nc.vector.tensor_tensor(pl[t][:], pw[t % 2][:], pv[t][:], MIN)
+            nc.vector.tensor_tensor(ph[t][:], board_a[:], pv[t][:], MAX)
+            nc.vector.tensor_tensor(pl[t][:], board_a[:], pv[t][:], MIN)
 
-        hid = keep.tile([P, 2, PACK, O], BF16, name="hid", tag="last", align_bytes=64)
-        out_rows = out.rearrange("(a p) d -> p a d", p=P)
-        for side, (board, places, weight) in enumerate(((ph, idx4, sa_sb), (pl, idx5, sb_sb))):
+        hid = keep.tile([P, 2, PACK, O], BF16, name="hid", tag="last_values", align_bytes=ALIGN)
+        out_rows = out.rearrange("(h p) d -> p h d", p=P)
+
+        def quantised_side(side, boards, offsets, weights):
             for t in range(PACK):
                 nc.scalar.activation(
-                    out=hid[:, side, t, :], in_=board[t][:].indirect(places[:]), func=COPY, scale=weight[:, t : t + 1]
+                    out=hid[:, side, t, :], in_=boards[t][:].indirect(offsets[:]), func=COPY, scale=weights[:, t : t + 1]
                 )
-            woven = keep.tile([P, O, PACK], BF16, name="woven%d" % side, align_bytes=64)
+            woven = keep.tile([P, O, PACK], BF16, name="woven%d" % side, align_bytes=ALIGN)
             for t0 in (0, 2):
                 nc.vector.tensor_copy(
-                    woven[:, :, t0 : t0 + 2].rearrange("p (c i) t -> p c t i", i=PACK),
-                    hid[:, side, t0 : t0 + 2, :].rearrange("p t (c i) -> p c t i", i=PACK),
+                    woven[:, :, t0 : t0 + 2].rearrange("p (c i) t -> p c t i", i=4),
+                    hid[:, side, t0 : t0 + 2, :].rearrange("p t (c i) -> p c t i", i=4),
                 )
-            codes = keep.tile([P, O], U32, name="codes%d" % side, align_bytes=64)
-            scales = keep.tile([P, O], U8, name="scales%d" % side, align_bytes=64)
+            codes = keep.tile([P, O], U32, name="codes%d" % side, align_bytes=ALIGN)
+            code_scales = keep.tile([P, O], U8, name="code_scales%d" % side, align_bytes=ALIGN)
             nc.vector.quantize_mx(
-                out=codes[:].bitcast(FP8X4), scales=scales[:], in_=woven[:].rearrange("p d t -> p (d t)")
+                out=codes[:].bitcast(FP8X4), scales=code_scales[:], in_=woven[:].rearrange("p d t -> p (d t)")
             )
-            cols = slice(O * side, O * (side + 1))
-            operands = [
-                dict(
-                    lhsT=vsw[:, 2 * P * half : 2 * P * (half + 1)].bitcast(FP4X4),
-                    lhsT_scale=vss[:, P * half : P * (half + 1)],
-                    rhs=codes[:].bitcast(FP8X4), rhs_scale=scales[:], start=True, stop=True,
-                )
-                for half in range(N // P)
-            ]
-            if side == 0:
-                y_win = psum_out.tile([P, N // P, O], F32, name="y_win")
-                for half in range(N // P):
-                    nc.tensor.matmul_mx(out=y_win[:, half, :], **operands[half])
-            else:
-                res_win = keep.tile([P, N // P, O], F32, name="res_win")
-                nc.scalar.copy(res_win[:], y_win[:])
-                nc.scalar.dma_start(out_rows[:, :, 0:O], res_win[:])
-                for half in range(N // P):
-                    acc = psum_out.tile([P, O], F32, name="y_lose%d" % half)
-                    nc.tensor.matmul_mx(out=acc[:], **operands[half])
-                    res = keep.tile([P, O], F32, name="res_lose%d" % half)
-                    if half == 1:
-                        nc.scalar.copy(res[:], acc[:])
-                        nc.scalar.dma_start(out_rows[:, half, cols], res[:])
-                    else:
-                        nc.vector.tensor_copy(res[:], acc[:])
-                        nc.sync.dma_start(out_rows[:, half, cols], res[:])
+            return codes, code_scales
+
+        def multiply_out(acc, h, codes, code_scales):
+            nc.tensor.matmul_mx(
+                out=acc,
+                lhsT=vsw[:, 2 * P * h : 2 * P * (h + 1)].bitcast(FP4X4), lhsT_scale=vss[:, P * h : P * (h + 1)],
+                rhs=codes[:].bitcast(FP8X4), rhs_scale=code_scales[:],
+                start=True, stop=True,
+            )
+
+        winners = quantised_side(0, ph, idx4, sa_tiles)
+        y_win = psum_out.tile([P, N // P, O], F32, name="y_win")
+        for h in range(N // P):
+            multiply_out(y_win[:, h, :], h, *winners)
+
+        losers = quantised_side(1, pl, idx5, sb_tiles)
+        res_win = keep.tile([P, N // P, O], F32, name="res_win")
+        nc.scalar.copy(res_win[:], y_win[:])
+        nc.scalar.dma_start(out_rows[:, :, 0:O], res_win[:])
+        for h, (copy_out, queue) in enumerate(((nc.vector.tensor_copy, nc.sync), (nc.scalar.copy, nc.scalar))):
+            y_lose = psum_out.tile([P, O], F32, name="y_lose%d" % h)
+            multiply_out(y_lose[:], h, *losers)
+            res_lose = keep.tile([P, O], F32, name="res_lose%d" % h)
+            copy_out(res_lose[:], y_lose[:])
+            queue.dma_start(out_rows[:, h, O:D], res_lose[:])

from contextlib import ExitStack

import concourse.mybir as mybir

K, J, R, T, C, O, D, N, S = 512, 256, 512, 1024, 512, 128, 256, 256, 1024
FLOPS = 2 * K * R * J * 2 + 2 * R * N * D

F32 = mybir.dt.float32
BF16 = mybir.dt.bfloat16
I32 = mybir.dt.int32
U32 = mybir.dt.uint32
U16 = mybir.dt.uint16
U8 = mybir.dt.uint8
FP8X4 = mybir.dt.float8_e4m3fn_x4
FP4X4 = mybir.dt.float4_e2m1fn_x4
COPY = mybir.ActivationFunctionType.Copy
MAX = mybir.AluOpType.max
MIN = mybir.AluOpType.min

P = 128
PACK = 4
QUAD = 32
QUADS = P // QUAD
HALF = J // 2
PER_COL = 16
ALIGN = 64
PW_BOARDS = 3

BOARD_BYTES = 4 * C
AT_XW_ALL = 0
AT_W2S_REST = 0
AT_W2S_1 = 4 * T - P
AT_WW_DEALT = AT_W2S_1 + BOARD_BYTES
AT_PW_2 = AT_WW_DEALT + 2 * N


def tile_picked_tokens_plain_twin_winnersides_store_plain_kernel(
    tc, xt_words, xt_scales, w_words, w_scales, w2_words, w2_scales, sa, sb, vs_words, vs_scales,
    offs, offs2, offs3, offs4, offs5, offs6, out,
):
    nc = tc.nc
    with ExitStack() as ctx:
        lists = ctx.enter_context(tc.tile_pool(name="lists", bufs=1))
        keep = ctx.enter_context(tc.tile_pool(name="keep", bufs=1))
        placed = ctx.enter_context(tc.tile_pool(name="placed", bufs=1))
        psum = ctx.enter_context(tc.psum_pool(name="psum", bufs=4))
        psum_out = ctx.enter_context(tc.psum_pool(name="psum_out", bufs=1))

        def load_list(src, name):
            offsets = lists.tile(list(src.shape), U16, name=name)
            nc.sync.dma_start(offsets[:], src)
            return offsets

        def live_rows(plane, q):
            return plane[QUAD * q : QUAD * q + PACK, :].bitcast(I32)

        def load_plane(queue, plane, scales):
            rows = scales[0].bitcast(I32)
            for q in range(QUADS):
                queue.dma_start(live_rows(plane, q), rows[PACK * q : PACK * (q + 1), :])

        def zeroed_board(pool, name, **place):
            board = pool.tile([P, C], F32, name=name, align_bytes=ALIGN, **place)
            nc.vector.memset(board[:], 0.0)
            return board

        def by_tile(matrix, t0, t1):
            return matrix.rearrange("p (m t) -> p t m", t=PACK)[:, t0:t1, :]

        xs_all = keep.tile([P, T], U8, name="xs_all", align_bytes=ALIGN, tag="xs_all")
        w2s_all = keep.tile([P, R], U8, name="w2s_all")
        ws_all = keep.tile([P, R], U8, name="ws_all")
        vss_all = keep.tile([P, S], U8, name="vss_all")
        for plane in (xs_all, w2s_all):
            nc.vector.memset(plane[:].bitcast(I32), 0)

        idx = load_list(offs, "idx")
        xw_all = placed.tile([P, T], I32, name="xw_all", align_bytes=ALIGN, offset=AT_XW_ALL)
        nc.sync.dma_start(xw_all[:], xt_words[0].rearrange("p c t -> p (c t)").bitcast(I32))
        w2s_staged = keep.tile([PACK, QUADS, R // 4], I32, name="w2s_staged")
        nc.scalar.dma_start(w2s_staged[:], w2_scales[0].bitcast(I32).rearrange("(q i) c -> i q c", i=PACK))
        load_plane(nc.scalar, xs_all, xt_scales)
        w2w_all = keep.tile([P, R], U16, name="w2w_all")
        nc.sync.dma_start(w2w_all[:].bitcast(I32), w2_words[0].bitcast(I32))

        idx3 = load_list(offs3, "idx3")
        idx6 = load_list(offs6, "idx6")
        ww_all = keep.tile([P, R], I32, name="ww_all")
        nc.sync.dma_start(ww_all[:], w_words[0].rearrange("p c t -> p (c t)").bitcast(I32))
        vsw_all = keep.tile([P, S], U16, name="vsw_all")
        nc.sync.dma_start(vsw_all[:].bitcast(I32), vs_words[0].bitcast(I32))
        pv = [zeroed_board(keep, "pv%d" % t) for t in range(2)]
        for plane, scales in ((ws_all, w_scales), (vss_all, vs_scales)):
            nc.vector.memset(plane[:].bitcast(I32), 0)
            load_plane(nc.sync, plane, scales)
        idx4 = load_list(offs4, "idx4")
        idx5 = load_list(offs5, "idx5")
        sa_tiles = keep.tile([P, PACK], F32, name="sa_tiles")
        nc.sync.dma_start(sa_tiles[:], sa.rearrange("(p t) o -> p (t o)", t=PACK))
        sb_tiles = keep.tile([P, PACK], F32, name="sb_tiles")
        nc.sync.dma_start(sb_tiles[:], sb.rearrange("(p t) o -> p (t o)", t=PACK))
        idx2 = load_list(offs2, "idx2")

        def gather_slots(dst, window, half):
            cols = HALF // PER_COL
            nc.vector.tensor_copy(dst, window.indirect(idx[:, cols * half : cols * (half + 1)]))

        def multiply(acc, words, scales, fmt, half):
            nc.tensor.matmul_mx(
                out=acc, lhsT=words.bitcast(fmt), lhsT_scale=scales,
                rhs=xw[half][:].bitcast(FP8X4), rhs_scale=xs[:, HALF * half : HALF * (half + 1)],
                start=True, stop=True,
            )

        def product(words, scales, fmt, name, tag=""):
            acc = psum.tile([P, J], F32, name="acc")
            for half in range(2):
                multiply(acc[:, HALF * half : HALF * (half + 1)], words, scales, fmt, half)
            values = keep.tile([P, J], F32, name=name, tag=tag, align_bytes=ALIGN)
            nc.vector.tensor_copy(values[:], acc[:])
            return values

        def scatter(board, offsets, values):
            nc.scalar.activation(out=board[:].indirect(offsets), in_=values[:], func=COPY)

        for q in range(QUADS):
            nc.vector.tensor_copy(live_rows(w2s_all, q), w2s_staged[:, q, :])
        w2s_0 = keep.tile([P, 1, P], U8, name="w2s_0", align_bytes=ALIGN)
        nc.vector.tensor_copy(w2s_0[:], by_tile(w2s_all[:], 0, 1))
        w2w_0 = keep.tile([P, 1, 2 * P], U8, name="w2w_0", align_bytes=ALIGN, tag="w2w_0")
        nc.scalar.copy(w2w_0[:].bitcast(U16), by_tile(w2w_all[:], 0, 1))
        w2w_rest = keep.tile([P, PACK - 1, 2 * P], U8, name="w2w_rest", align_bytes=ALIGN, tag="w2w_rest")
        nc.scalar.copy(w2w_rest[:].bitcast(U16), by_tile(w2w_all[:], 1, PACK))

        xw = [keep.tile([P, HALF], U32, name="xw_lo", align_bytes=ALIGN)]
        xs = keep.tile([P, J], U8, name="xs", align_bytes=ALIGN)
        gather_slots(xw[0][:], xw_all[:].bitcast(U32), 0)
        gather_slots(xs[:, 0:HALF], xs_all[:], 0)
        acc_lo = psum.tile([P, HALF], F32, name="acc")
        multiply(acc_lo[:], w2w_0[:, 0, :], w2s_0[:, 0, :], FP4X4, 0)
        b0_lo = keep.tile([P, HALF], F32, name="b0_lo")
        nc.scalar.activation(out=b0_lo[:], in_=acc_lo[:], func=COPY)
        scatter(pv[0], idx3[:, 0 : HALF // PER_COL], b0_lo)

        gather_slots(xs[:, HALF:J], xs_all[:], 1)
        xw.append(keep.tile([P, HALF], U32, name="xw_hi", align_bytes=ALIGN, tag="xs_all"))
        gather_slots(xw[1][:], xw_all[:].bitcast(U32), 1)
        acc_hi = psum.tile([P, HALF], F32, name="acc")
        multiply(acc_hi[:], w2w_0[:, 0, :], w2s_0[:, 0, :], FP4X4, 1)
        b0_hi = keep.tile([P, HALF], F32, name="b0_hi")
        nc.vector.tensor_copy(b0_hi[:], acc_hi[:])
        scatter(pv[0], idx3[:, HALF // PER_COL : J // PER_COL], b0_hi)

        w2s_1 = placed.tile([P, 1, P], U8, name="w2s_1", align_bytes=ALIGN, offset=AT_W2S_1)
        nc.vector.tensor_copy(w2s_1[:], by_tile(w2s_all[:], 1, 2))
        w2s_rest = placed.tile([P, 2, P], U8, name="w2s_rest", align_bytes=ALIGN, offset=AT_W2S_REST)
        nc.vector.tensor_copy(w2s_rest[:], by_tile(w2s_all[:], 2, PACK))
        scatter(pv[1], idx3[:], product(w2w_rest[:, 0, :], w2s_1[:, 0, :], FP4X4, "b1"))
        b_late = [product(w2w_rest[:, t - 1, :], w2s_rest[:, t - 2, :], FP4X4, "b%d" % t) for t in (2, 3)]
        pv.append(zeroed_board(keep, "pv2", tag="w2w_0"))
        pv.append(zeroed_board(placed, "pv3", offset=AT_W2S_1))
        for t in (2, 3):
            scatter(pv[t], idx3[:], b_late[t - 2])

        ws_dealt = keep.tile([P, PACK, P], U8, name="ws_dealt", align_bytes=ALIGN, tag="ws_dealt")
        nc.vector.tensor_copy(ws_dealt[:], by_tile(ws_all[:], 0, PACK))
        ww_dealt = placed.tile([P, PACK, P], I32, name="ww_dealt", align_bytes=ALIGN, offset=AT_WW_DEALT)
        nc.vector.tensor_copy(ww_dealt[:], by_tile(ww_all[:], 0, PACK))
        a = [
            product(ww_dealt[:, t, :], ws_dealt[:, t, :], FP8X4, "a%d" % t, "last_values" if t == PACK - 1 else "")
            for t in range(PACK)
        ]
        pw = [
            zeroed_board(keep, "pw0", tag="w2w_rest"),
            zeroed_board(placed, "pw1", offset=AT_W2S_REST),
            zeroed_board(placed, "pw2", offset=AT_PW_2),
        ]

        vsw = placed.tile([P, 2 * N], U8, name="vsw", align_bytes=ALIGN, offset=AT_WW_DEALT)
        vss = keep.tile([P, N], U8, name="vss", align_bytes=ALIGN, tag="ws_dealt")
        nc.vector.tensor_copy(vsw[:].bitcast(U16), vsw_all[:].indirect(idx6[:]))
        nc.vector.tensor_copy(vss[:], vss_all[:].indirect(idx6[:]))

        ph, pl = [], []
        for t in range(PACK):
            board_a = pw[t % PW_BOARDS]
            scatter(board_a, idx2[:], a[t])
            ph.append(keep.tile([P, C], F32, name="ph%d" % t))
            pl.append(keep.tile([P, C], F32, name="pl%d" % t))
            nc.vector.tensor_tensor(ph[t][:], board_a[:], pv[t][:], MAX)
            nc.vector.tensor_tensor(pl[t][:], board_a[:], pv[t][:], MIN)

        hid = keep.tile([P, 2, PACK, O], BF16, name="hid", tag="last_values", align_bytes=ALIGN)
        out_rows = out.rearrange("(h p) d -> p h d", p=P)

        def quantised_side(side, boards, offsets, weights):
            for t in range(PACK):
                nc.scalar.activation(
                    out=hid[:, side, t, :], in_=boards[t][:].indirect(offsets[:]), func=COPY, scale=weights[:, t : t + 1]
                )
            woven = keep.tile([P, O, PACK], BF16, name="woven%d" % side, align_bytes=ALIGN)
            for t0 in (0, 2):
                nc.vector.tensor_copy(
                    woven[:, :, t0 : t0 + 2].rearrange("p (c i) t -> p c t i", i=4),
                    hid[:, side, t0 : t0 + 2, :].rearrange("p t (c i) -> p c t i", i=4),
                )
            codes = keep.tile([P, O], U32, name="codes%d" % side, align_bytes=ALIGN)
            code_scales = keep.tile([P, O], U8, name="code_scales%d" % side, align_bytes=ALIGN)
            nc.vector.quantize_mx(
                out=codes[:].bitcast(FP8X4), scales=code_scales[:], in_=woven[:].rearrange("p d t -> p (d t)")
            )
            return codes, code_scales

        def multiply_out(acc, h, codes, code_scales):
            nc.tensor.matmul_mx(
                out=acc,
                lhsT=vsw[:, 2 * P * h : 2 * P * (h + 1)].bitcast(FP4X4), lhsT_scale=vss[:, P * h : P * (h + 1)],
                rhs=codes[:].bitcast(FP8X4), rhs_scale=code_scales[:],
                start=True, stop=True,
            )

        winners = quantised_side(0, ph, idx4, sa_tiles)
        y_win = psum_out.tile([P, N // P, O], F32, name="y_win")
        for h in range(N // P):
            multiply_out(y_win[:, h, :], h, *winners)

        losers = quantised_side(1, pl, idx5, sb_tiles)
        res_win = keep.tile([P, N // P, O], F32, name="res_win")
        nc.scalar.copy(res_win[:], y_win[:])
        nc.scalar.dma_start(out_rows[:, :, 0:O], res_win[:])
        for h, (copy_out, queue) in enumerate(((nc.vector.tensor_copy, nc.sync), (nc.scalar.copy, nc.scalar))):
            y_lose = psum_out.tile([P, O], F32, name="y_lose%d" % h)
            multiply_out(y_lose[:], h, *losers)
            res_lose = keep.tile([P, O], F32, name="res_lose%d" % h)
            copy_out(res_lose[:], y_lose[:])
            queue.dma_start(out_rows[:, h, O:D], res_lose[:])
